import numpy as np
import ml_dtypes


def mxq(x, axis, fmt="e4m3"):
    dtype, down = {"e4m3": (ml_dtypes.float8_e4m3fn, 7), "e5m2": (ml_dtypes.float8_e5m2, 14)}[fmt]
    v = np.moveaxis(np.asarray(x, np.float32).astype(ml_dtypes.bfloat16).astype(np.float64), axis, -1)
    blocks = v.reshape(v.shape[:-1] + (-1, 32))
    amax = np.abs(blocks).max(-1, keepdims=True)
    byte = np.maximum(np.where(amax > 0, np.frexp(amax)[1] - 1 + 127, 0) - down, 1)
    scale = np.exp2(byte - 127.0)
    codes = (blocks / scale).astype(np.float32).astype(dtype).astype(np.float64)
    return np.moveaxis((codes * scale).reshape(v.shape), -1, axis)


WIDE = False


def mx_kscale(k):
    if not WIDE:
        return np.ones(k)
    levels = np.array([10, -10, 5, -5, 0])
    if k % 512:
        return np.exp2(np.random.permutation(np.resize(levels, k // 32))).repeat(32)
    a = np.empty((k // 512, 16))
    for p in range(k // 512):
        a[p, :8] = np.random.permutation(np.resize(levels, 8))
        for g in range(8):
            far = levels[np.abs(levels - a[p, g]) >= 10]
            a[p, g + 8] = far[np.random.randint(len(far))]
    return np.exp2(a.ravel()).repeat(32)


def f64(x):
    return np.asarray(x).astype(np.float64)


def striped(idx):
    return np.tile(idx.reshape(-1, 16).T, (8, 1)).astype(np.uint16)


def unstriped(offs):
    return offs[:16].T.reshape(-1).astype(np.int64)


E2M1 = np.array([0.0, 0.5, 1.0, 1.5, 2.0, 3.0, 4.0, 6.0, -0.0, -0.5, -1.0, -1.5, -2.0, -3.0, -4.0, -6.0])


def pack_weight(w, fmt):
    k, n = w.shape
    w = f64(np.asarray(w, np.float32).astype(ml_dtypes.bfloat16)).reshape(k // 32, 32, n)
    amax = np.abs(w).max(1)
    if fmt == "e4m3":
        byte = np.frexp(amax)[1] - 1 + 127 - 7
    else:
        mant, ex = np.frexp(amax / 6.0)
        byte = np.where(mant > 0.5, ex, ex - 1) + 127
    byte = np.clip(np.where(amax > 0, byte, 1), 1, 254)
    scaled = (w * np.exp2(127.0 - byte)[:, None, :]).reshape(k, n).astype(np.float32)
    by_word = np.ascontiguousarray(scaled.reshape(k // 512, 128, 4, n).transpose(0, 1, 3, 2))
    if fmt == "e4m3":
        words = by_word.astype(ml_dtypes.float8_e4m3fn).view(np.uint8)
    else:
        c = by_word.astype(ml_dtypes.float4_e2m1fn).view(np.uint8) & 0xF
        words = (c[..., 0::2] | (c[..., 1::2] << 4)).reshape(k // 512, 128, 2 * n)
    return np.ascontiguousarray(words), np.ascontiguousarray(byte.astype(np.uint8).reshape(k // 512, 16, n))


def unpack_weight(words, scales, fmt):
    g, _, n = scales.shape
    words = np.ascontiguousarray(words).reshape(g, 128, n, -1)
    if fmt == "e4m3":
        vals = words.view(ml_dtypes.float8_e4m3fn).astype(np.float64)
    else:
        nib = np.empty((g, 128, n, 4), np.uint8)
        nib[..., 0::2] = words & 0xF
        nib[..., 1::2] = words >> 4
        vals = E2M1[nib]
    vals = vals * np.repeat(np.exp2(scales.astype(np.float64) - 127.0), 8, axis=1)[..., None]
    return vals.transpose(0, 1, 3, 2).reshape(g * 512, n)


def gelu(v):
    return 0.5 * v * (1.0 + np.tanh(np.sqrt(2.0 / np.pi) * (v + 0.044715 * v**3)))


K, T, S, H, T3, S2, P = 1024, 4096, 1024, 512, 2048, 1024, 512


def setup_inputs():
    n = np.random.standard_normal
    s = mx_kscale(K)[:, None]
    u = mx_kscale(H)[:, None]
    d = {}
    d["tab_words"], d["tab_scales"] = pack_weight(n((K, T)) * s, "e4m3")
    d["offs"] = striped(np.random.permutation(T)[:S])
    d["tab2_words"], d["tab2_scales"] = pack_weight(n((H, T3)) / u / H ** 0.5, "e4m3")
    d["offs2"] = striped(np.random.permutation(T3)[:S2])
    d["pos1"] = striped(np.random.permutation(S)[:P])
    d["pos2"] = striped(np.random.permutation(S)[:P])
    d["w1"] = (1.5 * n((K, H)) / s / K ** 0.5).astype(np.float32)
    d["w4_words"], d["w4_scales"] = pack_weight(n((K, H)) / s * u.T / K ** 0.5, "e2m1")
    d["w3"] = (0.6 * n((K, H)) / s * u.T / K ** 0.5).astype(np.float32)
    d["amin"] = (0.9 * n((S2, P))).astype(np.float32)
    return d


def reference(tab_words, tab_scales, offs, tab2_words, tab2_scales, offs2, pos1, pos2, w1, w4_words, w4_scales, w3, amin):
    v = unpack_weight(tab_words, tab_scales, "e4m3")[:, unstriped(offs)]
    v2 = unpack_weight(tab2_words, tab2_scales, "e4m3")[:, unstriped(offs2)]
    w4 = unpack_weight(w4_words, w4_scales, "e2m1")
    s = mxq(f64(w1), 0, "e4m3").T @ v
    b = w4.T @ v
    d = mxq(f64(w3), 0, "e4m3").T @ v
    h = b * np.tanh(s) + d * np.abs(s)
    e = v2.T @ mxq(h, 0, "e4m3")
    e1 = e[:, unstriped(pos1)]
    e2 = e[:, unstriped(pos2)]
    return np.maximum(np.maximum(e1, e2), f64(amin))

@@ -1,0 +1,267 @@
+from contextlib import ExitStack
+
+import concourse.mybir as mybir
+
+K, T, S, H, T3, S2, J = 1024, 4096, 1024, 512, 2048, 1024, 512
+FLOPS = 2 * (3 * K * H * S + H * S2 * S)
+
+F32 = mybir.dt.float32
+BF16 = mybir.dt.bfloat16
+I32 = mybir.dt.int32
+U32 = mybir.dt.uint32
+U16 = mybir.dt.uint16
+U8 = mybir.dt.uint8
+FP8X4 = mybir.dt.float8_e4m3fn_x4
+FP4X4 = mybir.dt.float4_e2m1fn_x4
+ALU = mybir.AluOpType
+ACT = mybir.ActivationFunctionType
+
+P = 128
+PACK = 4
+PASSES = K // (P * PACK)
+UNIT = 128
+UNITS = S // UNIT
+HALF = 512
+ROW_TILES = S2 // P
+
+
+def tile_list_pane_glass_scores_kernel(
+    tc, tab_words, tab_scales, offs, tab2_words, tab2_scales, offs2, pos1, pos2, w1, w4_words, w4_scales, w3, amin, out
+):
+    nc = tc.nc
+    with ExitStack() as ctx:
+        keep = ctx.enter_context(tc.tile_pool(name="keep", bufs=1))
+        ring = ctx.enter_context(tc.tile_pool(name="ring", bufs=3))
+        psum = ctx.enter_context(tc.psum_pool(name="psum", bufs=8))
+
+        def kept(shape, dtype, name):
+            return keep.tile(shape, dtype, name=name, align_bytes=64)
+
+        offs_sb = keep.tile([P, S // 16], U16, name="offs_sb")
+        offs2_sb = keep.tile([P, S2 // 16], U16, name="offs2_sb")
+        pos1_sb = keep.tile([P, J // 16], U16, name="pos1_sb")
+        pos2_sb = keep.tile([P, J // 16], U16, name="pos2_sb")
+
+        tab_sc = kept([P, PASSES, T], U8, "tab_sc")
+        w4_sc = kept([P, PASSES, H], U8, "w4_sc")
+        tab2_sc = kept([P, 1, T3], U8, "tab2_sc")
+        for plane in (tab_sc, w4_sc, tab2_sc):
+            nc.vector.memset(plane[:].bitcast(I32), 0)
+
+        warm = kept([P, 8], F32, "warm")
+        warm2 = kept([P, 8], F32, "warm2")
+        nc.gpsimd.memset(warm[:], 0.0)
+        nc.scalar.activation(warm2[:], warm[:], ACT.Tanh)
+
+        def load_scales(plane, scales):
+            for quad in range(4):
+                nc.sync.dma_start(
+                    out=plane[32 * quad : 32 * quad + 4, :, :].bitcast(I32),
+                    in_=scales[:, 4 * quad : 4 * quad + 4, :].rearrange("a r n -> r a n").bitcast(I32),
+                )
+
+        def load_weight(w, a, name):
+            raw = kept([P, PACK, H], F32, name)
+            rows = w[a * P * PACK : (a + 1) * P * PACK, :]
+            nc.sync.dma_start(out=raw[:], in_=rows.rearrange("(p j) c -> p j c", j=PACK))
+            return raw
+
+        def load_words(words, width, name):
+            tile = kept([P, width], I32, name)
+            nc.sync.dma_start(out=tile[:], in_=words.rearrange("p n i -> p (n i)").bitcast(I32))
+            return tile
+
+        nc.sync.dma_start(offs_sb[:], offs)
+        w4_raw = kept([P, PASSES, 2 * H], U8, "w4_raw")
+        nc.sync.dma_start(out=w4_raw[:].bitcast(I32), in_=w4_words.rearrange("a p n -> p a n").bitcast(I32))
+        w1_raw = [load_weight(w1, 0, "w1_raw0")]
+        load_scales(tab_sc, tab_scales)
+        w1_raw.append(load_weight(w1, 1, "w1_raw1"))
+        load_scales(w4_sc, w4_scales)
+        tab_w = [load_words(tab_words[0], T, "tab_w0")]
+        nc.sync.dma_start(offs2_sb[:], offs2)
+        load_scales(tab2_sc, tab2_scales)
+        tab_w.append(load_words(tab_words[1], T, "tab_w1"))
+        w3_raw = [load_weight(w3, a, "w3_raw%d" % a) for a in range(PASSES)]
+        tab2_w = load_words(tab2_words[0], T3, "tab2_w")
+        nc.sync.dma_start(pos1_sb[:], pos1)
+        nc.sync.dma_start(pos2_sb[:], pos2)
+        amin_sb = []
+        for half in range(2):
+            tile = kept([P, ROW_TILES // 2, J], F32, "amin%d" % half)
+            rows = amin[half * HALF : (half + 1) * HALF, :]
+            nc.sync.dma_start(out=tile[:], in_=rows.rearrange("(m p) j -> p m j", p=P))
+            amin_sb.append(tile)
+
+        def round_weight(raw, name):
+            grouped = kept([P, PACK, P, PACK], BF16, name)
+            nc.scalar.copy(
+                grouped[:].rearrange("p t q j -> p q j t"),
+                raw[:].rearrange("p j (q t) -> p q j t", t=PACK),
+            )
+            return grouped
+
+        def quantize_weight(grouped, name):
+            codes = kept([P, H], U32, name + "_codes")
+            scales = kept([P, H], U8, name + "_scales")
+            nc.vector.quantize_mx(
+                out=codes[:].bitcast(FP8X4), scales=scales[:], in_=grouped[:].rearrange("p t q j -> p (t q j)")
+            )
+            return codes, scales
+
+        def gather(window, offsets, count, dtype, name):
+            picked = kept([P, count], dtype, name)
+            nc.vector.tensor_copy(picked[:], window.indirect(offsets))
+            return picked
+
+        w4_codes = kept([P, PASSES, 2 * H], U8, "w4_codes")
+        nc.vector.tensor_copy(
+            w4_codes[:].bitcast(U16).rearrange("p a (t q) -> p a q t", t=PACK),
+            w4_raw[:].bitcast(U16).rearrange("p a (q t) -> p a q t", t=PACK),
+        )
+        w1_bf = [round_weight(w1_raw[a], "w1_bf%d" % a) for a in range(PASSES)]
+        v_sc = [gather(tab_sc[:, a, :], offs_sb[:], S, U8, "v_sc%d" % a) for a in range(PASSES)]
+        w1_q = [quantize_weight(w1_bf[a], "w1_%d" % a) for a in range(PASSES)]
+
+        w4_dealt = kept([P, PASSES, H], U8, "w4_dealt")
+        nc.vector.tensor_copy(
+            w4_dealt[:].rearrange("p a (t q) -> p a q t", t=PACK),
+            w4_sc[:].rearrange("p a (q t) -> p a q t", t=PACK),
+        )
+
+        def gather_words(a):
+            return [
+                gather(
+                    tab_w[a][:].bitcast(U32),
+                    offs_sb[:, half * HALF // 16 : (half + 1) * HALF // 16],
+                    HALF,
+                    U32,
+                    "v_w%d_%d" % (a, half),
+                )
+                for half in range(S // HALF)
+            ]
+
+        v_w = [gather_words(0)]
+        v2_sc = gather(tab2_sc[:, 0, :], offs2_sb[:], S2, U8, "v2_sc")
+        v_w.append(gather_words(1))
+
+        def fp8_weight(w_q):
+            def pick(a, t):
+                codes, scales = w_q[a]
+                cols = slice(t * P, (t + 1) * P)
+                return codes[:, cols].bitcast(FP8X4), scales[:, cols]
+
+            return pick
+
+        def fp4_weight(a, t):
+            return (
+                w4_codes[:, a, 2 * t * P : 2 * (t + 1) * P].bitcast(FP4X4),
+                w4_dealt[:, a, t * P : (t + 1) * P],
+            )
+
+        def first_product(pick, u):
+            acc = psum.tile([P, PACK, UNIT], F32, name="acc", tag="bank")
+            half, first = divmod(u * UNIT, HALF)
+            for a in range(PASSES):
+                for t in range(PACK):
+                    codes, scales = pick(a, t)
+                    nc.tensor.matmul_mx(
+                        out=acc[:, t, :],
+                        lhsT=codes,
+                        lhsT_scale=scales,
+                        rhs=v_w[a][half][:, first : first + UNIT].bitcast(FP8X4),
+                        rhs_scale=v_sc[a][:, u * UNIT : (u + 1) * UNIT],
+                        start=(a == 0 and t == 0),
+                        stop=(a == PASSES - 1 and t == PACK - 1),
+                    )
+            return acc[:].rearrange("p t n -> p n t")
+
+        def woven(tile):
+            return tile[:].rearrange("p (n t) -> p n t", t=PACK)
+
+        left, size = [], []
+        w3_bf = []
+
+        def steer(u):
+            s_acc = first_product(fp8_weight(w1_q), u)
+            b_acc = first_product(fp4_weight, u)
+            left.append(kept([P, PACK * UNIT], F32, "left%d" % u))
+            size.append(kept([P, PACK * UNIT], F32, "size%d" % u))
+            nc.scalar.activation(woven(left[u]), s_acc, ACT.Tanh)
+            nc.scalar.activation(woven(size[u]), s_acc, ACT.Abs)
+            nc.vector.tensor_tensor(woven(left[u]), b_acc, woven(left[u]), ALU.mult)
+            if u < PASSES:
+                w3_bf.append(round_weight(w3_raw[u], "w3_bf%d" % u))
+
+        LEAD = 4
+        for u in range(LEAD):
+            steer(u)
+        w3_q = [quantize_weight(w3_bf[a], "w3_%d" % a) for a in range(PASSES)]
+        v2_first = gather(tab2_w[:].bitcast(U32), offs2_sb[:, 0:16], 256, U32, "v2_first")
+
+        h_codes = kept([P, S], U32, "h_codes")
+        h_scales = kept([P, S], U8, "h_scales")
+        h_bf = {}
+
+        def scale_right(u):
+            d_acc = first_product(fp8_weight(w3_q), u)
+            nc.vector.tensor_tensor(woven(size[u]), d_acc, woven(size[u]), ALU.mult)
+
+        def add_halves(u):
+            h_bf[u] = ring.tile([P, PACK * UNIT], BF16, name="h_bf", align_bytes=64)
+            nc.vector.tensor_tensor(h_bf[u][:], left[u][:], size[u][:], ALU.add)
+
+        def quantize_h(u):
+            cols = slice(u * UNIT, (u + 1) * UNIT)
+            nc.vector.quantize_mx(out=h_codes[:, cols].bitcast(FP8X4), scales=h_scales[:, cols], in_=h_bf[u][:])
+
+        for step in range(UNITS + 2):
+            if step < UNITS:
+                scale_right(step)
+            if step + LEAD < UNITS:
+                steer(step + LEAD)
+            if 0 <= step - 2:
+                quantize_h(step - 2)
+            if 0 <= step - 1 < UNITS:
+                add_halves(step - 1)
+        v2_rest = gather(tab2_w[:].bitcast(U32), offs2_sb[:, 16:64], S2 - 256, U32, "v2_rest")
+
+        def scores(m):
+            e_sb = ring.tile([P, S], F32, name="e_sb")
+            if m < 2:
+                lhs = v2_first[:, m * P : (m + 1) * P]
+            else:
+                lhs = v2_rest[:, (m - 2) * P : (m - 1) * P]
+            edges = (0, 512, 768, 896, 1024) if m == 0 else (0, 512, 1024)
+            for first, last in zip(edges, edges[1:]):
+                cols = slice(first, last)
+                acc = psum.tile([P, last - first], F32, name="e_acc", tag="bank")
+                nc.tensor.matmul_mx(
+                    out=acc[:],
+                    lhsT=lhs.bitcast(FP8X4),
+                    lhsT_scale=v2_sc[:, m * P : (m + 1) * P],
+                    rhs=h_codes[:, cols].bitcast(FP8X4),
+                    rhs_scale=h_scales[:, cols],
+                    start=True,
+                    stop=True,
+                )
+                nc.scalar.copy(e_sb[:, cols], acc[:])
+            return e_sb
+
+        pending = None
+        for m in range(ROW_TILES + 1):
+            if m < ROW_TILES:
+                e_sb = scores(m)
+                morning = ring.tile([P, J], F32, name="morning")
+                nc.vector.tensor_copy(morning[:], e_sb[:].indirect(pos1_sb[:]))
+            if pending is not None:
+                floored, evening = pending
+                best = ring.tile([P, J], F32, name="best")
+                nc.vector.tensor_tensor(best[:], floored[:], evening[:], ALU.max)
+                nc.sync.dma_start(out=out[(m - 1) * P : m * P, :], in_=best[:])
+            if m < ROW_TILES:
+                evening = ring.tile([P, J], F32, name="evening")
+                nc.vector.tensor_copy(evening[:], e_sb[:].indirect(pos2_sb[:]))
+                floored = ring.tile([P, J], F32, name="floored")
+                nc.vector.tensor_tensor(floored[:], morning[:], amin_sb[m // 4][:, m % 4, :], ALU.max)
+                pending = (floored, evening)

@@ -34,31 +34,31 @@ def tile_list_pane_glass_scores_kernel(
         ring = ctx.enter_context(tc.tile_pool(name="ring", bufs=3))
         psum = ctx.enter_context(tc.psum_pool(name="psum", bufs=8))
 
-        def kept(shape, dtype, name):
-            return keep.tile(shape, dtype, name=name, align_bytes=64)
+        def kept(shape, dtype, name, tag=None):
+            return keep.tile(shape, dtype, name=name, tag=tag or name, align_bytes=64)
 
         offs_sb = keep.tile([P, S // 16], U16, name="offs_sb")
         offs2_sb = keep.tile([P, S2 // 16], U16, name="offs2_sb")
         pos1_sb = keep.tile([P, J // 16], U16, name="pos1_sb")
         pos2_sb = keep.tile([P, J // 16], U16, name="pos2_sb")
 
-        tab_sc = kept([P, PASSES, T], U8, "tab_sc")
+        tab_sc = kept([P, T], U8, "tab_sc")
+        v_sc_low = kept([P, S], U8, "v_sc_low")
         w4_sc = kept([P, PASSES, H], U8, "w4_sc")
-        tab2_sc = kept([P, 1, T3], U8, "tab2_sc")
-        for plane in (tab_sc, w4_sc, tab2_sc):
+        tab2_sc = kept([P, T3], U8, "tab2_sc")
+        for plane in (tab_sc, w4_sc, tab2_sc, v_sc_low):
             nc.vector.memset(plane[:].bitcast(I32), 0)
 
         warm = kept([P, 8], F32, "warm")
         warm2 = kept([P, 8], F32, "warm2")
-        nc.gpsimd.memset(warm[:], 0.0)
+        nc.vector.memset(warm[:], 0.0)
         nc.scalar.activation(warm2[:], warm[:], ACT.Tanh)
 
-        def load_scales(plane, scales):
-            for quad in range(4):
-                nc.sync.dma_start(
-                    out=plane[32 * quad : 32 * quad + 4, :, :].bitcast(I32),
-                    in_=scales[:, 4 * quad : 4 * quad + 4, :].rearrange("a r n -> r a n").bitcast(I32),
-                )
+
+        def gather(window, offsets, count, dtype, name, tag=None):
+            picked = kept([P, count], dtype, name, tag)
+            nc.vector.tensor_copy(picked[:], window.indirect(offsets))
+            return picked
 
         def load_weight(w, a, name):
             raw = kept([P, PACK, H], F32, name)
@@ -72,17 +72,36 @@ def tile_list_pane_glass_scores_kernel(
             return tile
 
         nc.sync.dma_start(offs_sb[:], offs)
+        nc.sync.dma_start(offs2_sb[:], offs2)
         w4_raw = kept([P, PASSES, 2 * H], U8, "w4_raw")
         nc.sync.dma_start(out=w4_raw[:].bitcast(I32), in_=w4_words.rearrange("a p n -> p a n").bitcast(I32))
         w1_raw = [load_weight(w1, 0, "w1_raw0")]
-        load_scales(tab_sc, tab_scales)
+        for quad in range(4):
+            nc.sync.dma_start(
+                out=tab_sc[32 * quad : 32 * quad + 8, :].bitcast(I32),
+                in_=tab_scales[:, 4 * quad : 4 * quad + 4, :].bitcast(I32),
+            )
         w1_raw.append(load_weight(w1, 1, "w1_raw1"))
-        load_scales(w4_sc, w4_scales)
+        for quad in range(4):
+            nc.sync.dma_start(
+                out=w4_sc[32 * quad : 32 * quad + 4, :, :].bitcast(I32),
+                in_=w4_scales[:, 4 * quad : 4 * quad + 4, :].rearrange("a r n -> r a n").bitcast(I32),
+            )
+        w3_raw = [load_weight(w3, 0, "w3_raw0")]
+        for quad in range(4):
+            nc.sync.dma_start(
+                out=tab2_sc[32 * quad + 8 : 32 * quad + 12, :].bitcast(I32),
+                in_=tab2_scales[0, 4 * quad : 4 * quad + 4, :].bitcast(I32),
+            )
         tab_w = [load_words(tab_words[0], T, "tab_w0")]
-        nc.sync.dma_start(offs2_sb[:], offs2)
-        load_scales(tab2_sc, tab2_scales)
+        v_sc = gather(tab_sc[:], offs_sb[:], S, U8, "v_sc")
+        for quad in range(4):
+            nc.sync.dma_start(
+                out=v_sc_low[32 * quad : 32 * quad + 4, :].bitcast(I32),
+                in_=v_sc[32 * quad + 4 : 32 * quad + 8, :].bitcast(I32),
+            )
         tab_w.append(load_words(tab_words[1], T, "tab_w1"))
-        w3_raw = [load_weight(w3, a, "w3_raw%d" % a) for a in range(PASSES)]
+        w3_raw.append(load_weight(w3, 1, "w3_raw1"))
         tab2_w = load_words(tab2_words[0], T3, "tab2_w")
         nc.sync.dma_start(pos1_sb[:], pos1)
         nc.sync.dma_start(pos2_sb[:], pos2)
@@ -93,9 +112,9 @@ def tile_list_pane_glass_scores_kernel(
             nc.sync.dma_start(out=tile[:], in_=rows.rearrange("(m p) j -> p m j", p=P))
             amin_sb.append(tile)
 
-        def round_weight(raw, name):
+        def round_weight(raw, name, copy):
             grouped = kept([P, PACK, P, PACK], BF16, name)
-            nc.scalar.copy(
+            copy(
                 grouped[:].rearrange("p t q j -> p q j t"),
                 raw[:].rearrange("p j (q t) -> p q j t", t=PACK),
             )
@@ -109,18 +128,14 @@ def tile_list_pane_glass_scores_kernel(
             )
             return codes, scales
 
-        def gather(window, offsets, count, dtype, name):
-            picked = kept([P, count], dtype, name)
-            nc.vector.tensor_copy(picked[:], window.indirect(offsets))
-            return picked
-
         w4_codes = kept([P, PASSES, 2 * H], U8, "w4_codes")
         nc.vector.tensor_copy(
             w4_codes[:].bitcast(U16).rearrange("p a (t q) -> p a q t", t=PACK),
             w4_raw[:].bitcast(U16).rearrange("p a (q t) -> p a q t", t=PACK),
         )
-        w1_bf = [round_weight(w1_raw[a], "w1_bf%d" % a) for a in range(PASSES)]
-        v_sc = [gather(tab_sc[:, a, :], offs_sb[:], S, U8, "v_sc%d" % a) for a in range(PASSES)]
+        w1_bf = [round_weight(w1_raw[a], "w1_bf%d" % a, nc.scalar.copy) for a in range(PASSES)]
+        packed_planes = (v_sc[:], v_sc[4:P, :])
+        low_planes = (v_sc[:], v_sc_low[:])
         w1_q = [quantize_weight(w1_bf[a], "w1_%d" % a) for a in range(PASSES)]
 
         w4_dealt = kept([P, PASSES, H], U8, "w4_dealt")
@@ -128,6 +143,8 @@ def tile_list_pane_glass_scores_kernel(
             w4_dealt[:].rearrange("p a (t q) -> p a q t", t=PACK),
             w4_sc[:].rearrange("p a (q t) -> p a q t", t=PACK),
         )
+        v2_sc = gather(tab2_sc[:], offs2_sb[:], S2, U8, "v2_sc")
+        w3_q = [quantize_weight(round_weight(w3_raw[0], "w3_bf0", nc.scalar.copy), "w3_0")]
 
         def gather_words(a):
             return [
@@ -141,9 +158,8 @@ def tile_list_pane_glass_scores_kernel(
                 for half in range(S // HALF)
             ]
 
-        v_w = [gather_words(0)]
-        v2_sc = gather(tab2_sc[:, 0, :], offs2_sb[:], S2, U8, "v2_sc")
-        v_w.append(gather_words(1))
+        v_w = [gather_words(a) for a in range(PASSES)]
+        w3_late = round_weight(w3_raw[1], "w3_bf1", nc.vector.tensor_copy)
 
         def fp8_weight(w_q):
             def pick(a, t):
@@ -159,7 +175,7 @@ def tile_list_pane_glass_scores_kernel(
                 w4_dealt[:, a, t * P : (t + 1) * P],
             )
 
-        def first_product(pick, u):
+        def first_product(pick, planes, u):
             acc = psum.tile([P, PACK, UNIT], F32, name="acc", tag="bank")
             half, first = divmod(u * UNIT, HALF)
             for a in range(PASSES):
@@ -170,7 +186,7 @@ def tile_list_pane_glass_scores_kernel(
                         lhsT=codes,
                         lhsT_scale=scales,
                         rhs=v_w[a][half][:, first : first + UNIT].bitcast(FP8X4),
-                        rhs_scale=v_sc[a][:, u * UNIT : (u + 1) * UNIT],
+                        rhs_scale=planes[a][:, u * UNIT : (u + 1) * UNIT],
                         start=(a == 0 and t == 0),
                         stop=(a == PASSES - 1 and t == PACK - 1),
                     )
@@ -179,59 +195,63 @@ def tile_list_pane_glass_scores_kernel(
         def woven(tile):
             return tile[:].rearrange("p (n t) -> p n t", t=PACK)
 
-        left, size = [], []
-        w3_bf = []
-
-        def steer(u):
-            s_acc = first_product(fp8_weight(w1_q), u)
-            b_acc = first_product(fp4_weight, u)
-            left.append(kept([P, PACK * UNIT], F32, "left%d" % u))
-            size.append(kept([P, PACK * UNIT], F32, "size%d" % u))
-            nc.scalar.activation(woven(left[u]), s_acc, ACT.Tanh)
-            nc.scalar.activation(woven(size[u]), s_acc, ACT.Abs)
-            nc.vector.tensor_tensor(woven(left[u]), b_acc, woven(left[u]), ALU.mult)
-            if u < PASSES:
-                w3_bf.append(round_weight(w3_raw[u], "w3_bf%d" % u))
-
-        LEAD = 4
-        for u in range(LEAD):
-            steer(u)
-        w3_q = [quantize_weight(w3_bf[a], "w3_%d" % a) for a in range(PASSES)]
-        v2_first = gather(tab2_w[:].bitcast(U32), offs2_sb[:, 0:16], 256, U32, "v2_first")
-
         h_codes = kept([P, S], U32, "h_codes")
         h_scales = kept([P, S], U8, "h_scales")
-        h_bf = {}
+        left, right, h_bf = {}, {}, {}
+
+        def steer(u):
+            s_acc = first_product(fp8_weight(w1_q), packed_planes, u)
+            b_acc = first_product(fp4_weight, low_planes, u)
+            left[u] = kept([P, PACK * UNIT], F32, "left%d" % u)
+            right[u] = kept([P, PACK * UNIT], F32, "right%d" % u)
+            nc.scalar.activation(woven(left[u]), s_acc, ACT.Tanh)
+            nc.scalar.activation(woven(right[u]), s_acc, ACT.Abs)
+            nc.vector.tensor_tensor(woven(left[u]), b_acc, woven(left[u]), ALU.mult)
 
         def scale_right(u):
-            d_acc = first_product(fp8_weight(w3_q), u)
-            nc.vector.tensor_tensor(woven(size[u]), d_acc, woven(size[u]), ALU.mult)
+            d_acc = first_product(fp8_weight(w3_q), packed_planes, u)
+            nc.vector.tensor_tensor(woven(right[u]), d_acc, woven(right[u]), ALU.mult)
 
-        def add_halves(u):
-            h_bf[u] = ring.tile([P, PACK * UNIT], BF16, name="h_bf", align_bytes=64)
-            nc.vector.tensor_tensor(h_bf[u][:], left[u][:], size[u][:], ALU.add)
+        def add_terms(u, engine):
+            h_bf[u] = kept([P, PACK * UNIT], BF16, "h_bf%d" % u)
+            engine.tensor_tensor(h_bf[u][:], left[u][:], right[u][:], ALU.add)
 
         def quantize_h(u):
             cols = slice(u * UNIT, (u + 1) * UNIT)
             nc.vector.quantize_mx(out=h_codes[:, cols].bitcast(FP8X4), scales=h_scales[:, cols], in_=h_bf[u][:])
 
-        for step in range(UNITS + 2):
-            if step < UNITS:
-                scale_right(step)
-            if step + LEAD < UNITS:
-                steer(step + LEAD)
-            if 0 <= step - 2:
-                quantize_h(step - 2)
-            if 0 <= step - 1 < UNITS:
-                add_halves(step - 1)
-        v2_rest = gather(tab2_w[:].bitcast(U32), offs2_sb[:, 16:64], S2 - 256, U32, "v2_rest")
+        LEAD = 3
+        POOL_UNITS = 6
+        steer(0)
+        w3_q.append(quantize_weight(w3_late, "w3_1"))
+        for u in range(1, LEAD):
+            steer(u)
+        v2_first = gather(tab2_w[:].bitcast(U32), offs2_sb[:, 0:16], 256, U32, "v2_first")
+        for u in range(UNITS):
+            if u + LEAD < UNITS:
+                steer(u + LEAD)
+                if u >= 2:
+                    quantize_h(u - 2)
+            scale_right(u)
+            if u < POOL_UNITS:
+                add_terms(u, nc.gpsimd)
+        for u in range(max(UNITS - LEAD - 2, 0), POOL_UNITS - 1):
+            quantize_h(u)
+        for u in range(POOL_UNITS, UNITS):
+            add_terms(u, nc.vector)
+            quantize_h(u - 1)
+        quantize_h(UNITS - 1)
+        v2_mid = gather(tab2_w[:].bitcast(U32), offs2_sb[:, 16:48], 512, U32, "v2_mid", "v_w1_1")
+        v2_last = gather(tab2_w[:].bitcast(U32), offs2_sb[:, 48:64], 256, U32, "v2_last", "v_w0_1")
 
         def scores(m):
             e_sb = ring.tile([P, S], F32, name="e_sb")
             if m < 2:
                 lhs = v2_first[:, m * P : (m + 1) * P]
+            elif m < 6:
+                lhs = v2_mid[:, (m - 2) * P : (m - 1) * P]
             else:
-                lhs = v2_rest[:, (m - 2) * P : (m - 1) * P]
+                lhs = v2_last[:, (m - 6) * P : (m - 5) * P]
             edges = (0, 512, 768, 896, 1024) if m == 0 else (0, 512, 1024)
             for first, last in zip(edges, edges[1:]):
                 cols = slice(first, last)
@@ -239,7 +259,7 @@ def tile_list_pane_glass_scores_kernel(
                 nc.tensor.matmul_mx(
                     out=acc[:],
                     lhsT=lhs.bitcast(FP8X4),
-                    lhsT_scale=v2_sc[:, m * P : (m + 1) * P],
+                    lhsT_scale=v2_sc[8:P, m * P : (m + 1) * P],
                     rhs=h_codes[:, cols].bitcast(FP8X4),
                     rhs_scale=h_scales[:, cols],
                     start=True,
@@ -248,20 +268,29 @@ def tile_list_pane_glass_scores_kernel(
                 nc.scalar.copy(e_sb[:, cols], acc[:])
             return e_sb
 
+        def finish(m, floored, evening, cols):
+            best = ring.tile([P, cols.stop - cols.start], F32, name="best")
+            nc.vector.tensor_tensor(best[:], floored[:, cols], evening[:], ALU.max)
+            nc.sync.dma_start(out=out[m * P : (m + 1) * P, cols], in_=best[:])
+
+        def pick(e_sb, pos_sb, cols, name):
+            picked = ring.tile([P, cols.stop - cols.start], F32, name=name)
+            nc.vector.tensor_copy(picked[:], e_sb[:].indirect(pos_sb[:, cols.start // 16 : cols.stop // 16]))
+            return picked
+
+        whole = slice(0, J)
         pending = None
-        for m in range(ROW_TILES + 1):
-            if m < ROW_TILES:
-                e_sb = scores(m)
-                morning = ring.tile([P, J], F32, name="morning")
-                nc.vector.tensor_copy(morning[:], e_sb[:].indirect(pos1_sb[:]))
+        for m in range(ROW_TILES):
+            e_sb = scores(m)
+            morning = pick(e_sb, pos1_sb, whole, "morning")
             if pending is not None:
-                floored, evening = pending
-                best = ring.tile([P, J], F32, name="best")
-                nc.vector.tensor_tensor(best[:], floored[:], evening[:], ALU.max)
-                nc.sync.dma_start(out=out[(m - 1) * P : m * P, :], in_=best[:])
-            if m < ROW_TILES:
-                evening = ring.tile([P, J], F32, name="evening")
-                nc.vector.tensor_copy(evening[:], e_sb[:].indirect(pos2_sb[:]))
-                floored = ring.tile([P, J], F32, name="floored")
-                nc.vector.tensor_tensor(floored[:], morning[:], amin_sb[m // 4][:, m % 4, :], ALU.max)
-                pending = (floored, evening)
+                finish(*pending)
+            floored = ring.tile([P, J], F32, name="floored")
+            nc.vector.tensor_tensor(floored[:], morning[:], amin_sb[m // 4][:, m % 4, :], ALU.max)
+            if m < ROW_TILES - 1:
+                pending = (m, floored, pick(e_sb, pos2_sb, whole, "evening"), whole)
+            else:
+                halves = (slice(0, J // 2), slice(J // 2, J))
+                evenings = [pick(e_sb, pos2_sb, cols, "evening") for cols in halves]
+                for cols, evening in zip(halves, evenings):
+                    finish(m, floored, evening, cols)

@@ -76,29 +76,29 @@ def tile_list_pane_glass_scores_kernel(
         w4_raw = kept([P, PASSES, 2 * H], U8, "w4_raw")
         nc.sync.dma_start(out=w4_raw[:].bitcast(I32), in_=w4_words.rearrange("a p n -> p a n").bitcast(I32))
         w1_raw = [load_weight(w1, 0, "w1_raw0")]
-        for quad in range(4):
+        for quad in (0, 2, 1, 3):
             nc.sync.dma_start(
                 out=tab_sc[32 * quad : 32 * quad + 8, :].bitcast(I32),
                 in_=tab_scales[:, 4 * quad : 4 * quad + 4, :].bitcast(I32),
             )
         w1_raw.append(load_weight(w1, 1, "w1_raw1"))
-        for quad in range(4):
+        for r in range(4):
             nc.sync.dma_start(
-                out=w4_sc[32 * quad : 32 * quad + 4, :, :].bitcast(I32),
-                in_=w4_scales[:, 4 * quad : 4 * quad + 4, :].rearrange("a r n -> r a n").bitcast(I32),
+                out=w4_sc[r:P:32, :, :].bitcast(I32),
+                in_=w4_scales[:, r:16:4, :].rearrange("a q n -> q a n").bitcast(I32),
             )
         w3_raw = [load_weight(w3, 0, "w3_raw0")]
-        for quad in range(4):
+        for r in range(4):
             nc.sync.dma_start(
-                out=tab2_sc[32 * quad + 8 : 32 * quad + 12, :].bitcast(I32),
-                in_=tab2_scales[0, 4 * quad : 4 * quad + 4, :].bitcast(I32),
+                out=tab2_sc[8 + r : P : 32, :].bitcast(I32),
+                in_=tab2_scales[0, r:16:4, :].bitcast(I32),
             )
         tab_w = [load_words(tab_words[0], T, "tab_w0")]
         v_sc = gather(tab_sc[:], offs_sb[:], S, U8, "v_sc")
-        for quad in range(4):
+        for r in range(4):
             nc.sync.dma_start(
-                out=v_sc_low[32 * quad : 32 * quad + 4, :].bitcast(I32),
-                in_=v_sc[32 * quad + 4 : 32 * quad + 8, :].bitcast(I32),
+                out=v_sc_low[r:P:32, :].bitcast(I32),
+                in_=v_sc[4 + r : P : 32, :].bitcast(I32),
             )
         tab_w.append(load_words(tab_words[1], T, "tab_w1"))
         w3_raw.append(load_weight(w3, 1, "w3_raw1"))
@@ -130,8 +130,8 @@ def tile_list_pane_glass_scores_kernel(
 
         w4_codes = kept([P, PASSES, 2 * H], U8, "w4_codes")
         nc.vector.tensor_copy(
-            w4_codes[:].bitcast(U16).rearrange("p a (t q) -> p a q t", t=PACK),
-            w4_raw[:].bitcast(U16).rearrange("p a (q t) -> p a q t", t=PACK),
+            w4_codes[:].bitcast(U16).rearrange("p a (t q) -> p a t q", t=PACK),
+            w4_raw[:].bitcast(U16).rearrange("p a (q t) -> p a t q", t=PACK),
         )
         w1_bf = [round_weight(w1_raw[a], "w1_bf%d" % a, nc.scalar.copy) for a in range(PASSES)]
         packed_planes = (v_sc[:], v_sc[4:P, :])
@@ -140,8 +140,8 @@ def tile_list_pane_glass_scores_kernel(
 
         w4_dealt = kept([P, PASSES, H], U8, "w4_dealt")
         nc.vector.tensor_copy(
-            w4_dealt[:].rearrange("p a (t q) -> p a q t", t=PACK),
-            w4_sc[:].rearrange("p a (q t) -> p a q t", t=PACK),
+            w4_dealt[:].rearrange("p a (t q) -> p a t q", t=PACK),
+            w4_sc[:].rearrange("p a (q t) -> p a t q", t=PACK),
         )
         v2_sc = gather(tab2_sc[:], offs2_sb[:], S2, U8, "v2_sc")
         w3_q = [quantize_weight(round_weight(w3_raw[0], "w3_bf0", nc.scalar.copy), "w3_0")]
@@ -197,7 +197,8 @@ def tile_list_pane_glass_scores_kernel(
 
         h_codes = kept([P, S], U32, "h_codes")
         h_scales = kept([P, S], U8, "h_scales")
-        left, right, h_bf = {}, {}, {}
+        h_bf = kept([P, PACK * S], BF16, "h_bf")
+        left, right = {}, {}
 
         def steer(u):
             s_acc = first_product(fp8_weight(w1_q), packed_planes, u)
@@ -213,14 +214,17 @@ def tile_list_pane_glass_scores_kernel(
             nc.vector.tensor_tensor(woven(right[u]), d_acc, woven(right[u]), ALU.mult)
 
         def add_terms(u, engine):
-            h_bf[u] = kept([P, PACK * UNIT], BF16, "h_bf%d" % u)
-            engine.tensor_tensor(h_bf[u][:], left[u][:], right[u][:], ALU.add)
+            engine.tensor_tensor(h_bf[:, PACK * u * UNIT : PACK * (u + 1) * UNIT], left[u][:], right[u][:], ALU.add)
 
-        def quantize_h(u):
-            cols = slice(u * UNIT, (u + 1) * UNIT)
-            nc.vector.quantize_mx(out=h_codes[:, cols].bitcast(FP8X4), scales=h_scales[:, cols], in_=h_bf[u][:])
+        def quantize_h(first, last):
+            cols = slice(first * UNIT, last * UNIT)
+            nc.vector.quantize_mx(
+                out=h_codes[:, cols].bitcast(FP8X4),
+                scales=h_scales[:, cols],
+                in_=h_bf[:, PACK * cols.start : PACK * cols.stop],
+            )
 
-        LEAD = 3
+        LEAD = 2
         POOL_UNITS = 6
         steer(0)
         w3_q.append(quantize_weight(w3_late, "w3_1"))
@@ -230,17 +234,15 @@ def tile_list_pane_glass_scores_kernel(
         for u in range(UNITS):
             if u + LEAD < UNITS:
                 steer(u + LEAD)
-                if u >= 2:
-                    quantize_h(u - 2)
             scale_right(u)
             if u < POOL_UNITS:
                 add_terms(u, nc.gpsimd)
-        for u in range(max(UNITS - LEAD - 2, 0), POOL_UNITS - 1):
-            quantize_h(u)
-        for u in range(POOL_UNITS, UNITS):
-            add_terms(u, nc.vector)
-            quantize_h(u - 1)
-        quantize_h(UNITS - 1)
+        quantize_h(0, 4)
+        add_terms(6, nc.vector)
+        add_terms(7, nc.vector)
+        quantize_h(4, 6)
+        quantize_h(6, 7)
+        quantize_h(7, 8)
         v2_mid = gather(tab2_w[:].bitcast(U32), offs2_sb[:, 16:48], 512, U32, "v2_mid", "v_w1_1")
         v2_last = gather(tab2_w[:].bitcast(U32), offs2_sb[:, 48:64], 256, U32, "v2_last", "v_w0_1")
 

from contextlib import ExitStack

import concourse.mybir as mybir

K, T, S, H, T3, S2, J = 1024, 4096, 1024, 512, 2048, 1024, 512
FLOPS = 2 * (3 * K * H * S + H * S2 * S)

F32 = mybir.dt.float32
BF16 = mybir.dt.bfloat16
I32 = mybir.dt.int32
U32 = mybir.dt.uint32
U16 = mybir.dt.uint16
U8 = mybir.dt.uint8
FP8X4 = mybir.dt.float8_e4m3fn_x4
FP4X4 = mybir.dt.float4_e2m1fn_x4
ALU = mybir.AluOpType
ACT = mybir.ActivationFunctionType

P = 128
PACK = 4
PASSES = K // (P * PACK)
UNIT = 128
UNITS = S // UNIT
HALF = 512
ROW_TILES = S2 // P


def tile_list_pane_glass_scores_kernel(
    tc, tab_words, tab_scales, offs, tab2_words, tab2_scales, offs2, pos1, pos2, w1, w4_words, w4_scales, w3, amin, out
):
    nc = tc.nc
    with ExitStack() as ctx:
        keep = ctx.enter_context(tc.tile_pool(name="keep", bufs=1))
        ring = ctx.enter_context(tc.tile_pool(name="ring", bufs=3))
        psum = ctx.enter_context(tc.psum_pool(name="psum", bufs=8))

        def kept(shape, dtype, name, tag=None):
            return keep.tile(shape, dtype, name=name, tag=tag or name, align_bytes=64)

        offs_sb = keep.tile([P, S // 16], U16, name="offs_sb")
        offs2_sb = keep.tile([P, S2 // 16], U16, name="offs2_sb")
        pos1_sb = keep.tile([P, J // 16], U16, name="pos1_sb")
        pos2_sb = keep.tile([P, J // 16], U16, name="pos2_sb")

        tab_sc = kept([P, T], U8, "tab_sc")
        v_sc_low = kept([P, S], U8, "v_sc_low")
        w4_sc = kept([P, PASSES, H], U8, "w4_sc")
        tab2_sc = kept([P, T3], U8, "tab2_sc")
        for plane in (tab_sc, w4_sc, tab2_sc, v_sc_low):
            nc.vector.memset(plane[:].bitcast(I32), 0)

        warm = kept([P, 8], F32, "warm")
        warm2 = kept([P, 8], F32, "warm2")
        nc.vector.memset(warm[:], 0.0)
        nc.scalar.activation(warm2[:], warm[:], ACT.Tanh)


        def gather(window, offsets, count, dtype, name, tag=None):
            picked = kept([P, count], dtype, name, tag)
            nc.vector.tensor_copy(picked[:], window.indirect(offsets))
            return picked

        def load_weight(w, a, name):
            raw = kept([P, PACK, H], F32, name)
            rows = w[a * P * PACK : (a + 1) * P * PACK, :]
            nc.sync.dma_start(out=raw[:], in_=rows.rearrange("(p j) c -> p j c", j=PACK))
            return raw

        def load_words(words, width, name):
            tile = kept([P, width], I32, name)
            nc.sync.dma_start(out=tile[:], in_=words.rearrange("p n i -> p (n i)").bitcast(I32))
            return tile

        nc.sync.dma_start(offs_sb[:], offs)
        nc.sync.dma_start(offs2_sb[:], offs2)
        w4_raw = kept([P, PASSES, 2 * H], U8, "w4_raw")
        nc.sync.dma_start(out=w4_raw[:].bitcast(I32), in_=w4_words.rearrange("a p n -> p a n").bitcast(I32))
        w1_raw = [load_weight(w1, 0, "w1_raw0")]
        for quad in (0, 2, 1, 3):
            nc.sync.dma_start(
                out=tab_sc[32 * quad : 32 * quad + 8, :].bitcast(I32),
                in_=tab_scales[:, 4 * quad : 4 * quad + 4, :].bitcast(I32),
            )
        w1_raw.append(load_weight(w1, 1, "w1_raw1"))
        for r in range(4):
            nc.sync.dma_start(
                out=w4_sc[r:P:32, :, :].bitcast(I32),
                in_=w4_scales[:, r:16:4, :].rearrange("a q n -> q a n").bitcast(I32),
            )
        w3_raw = [load_weight(w3, 0, "w3_raw0")]
        for r in range(4):
            nc.sync.dma_start(
                out=tab2_sc[8 + r : P : 32, :].bitcast(I32),
                in_=tab2_scales[0, r:16:4, :].bitcast(I32),
            )
        tab_w = [load_words(tab_words[0], T, "tab_w0")]
        v_sc = gather(tab_sc[:], offs_sb[:], S, U8, "v_sc")
        for r in range(4):
            nc.sync.dma_start(
                out=v_sc_low[r:P:32, :].bitcast(I32),
                in_=v_sc[4 + r : P : 32, :].bitcast(I32),
            )
        tab_w.append(load_words(tab_words[1], T, "tab_w1"))
        w3_raw.append(load_weight(w3, 1, "w3_raw1"))
        tab2_w = load_words(tab2_words[0], T3, "tab2_w")
        nc.sync.dma_start(pos1_sb[:], pos1)
        nc.sync.dma_start(pos2_sb[:], pos2)
        amin_sb = []
        for half in range(2):
            tile = kept([P, ROW_TILES // 2, J], F32, "amin%d" % half)
            rows = amin[half * HALF : (half + 1) * HALF, :]
            nc.sync.dma_start(out=tile[:], in_=rows.rearrange("(m p) j -> p m j", p=P))
            amin_sb.append(tile)

        def round_weight(raw, name, copy):
            grouped = kept([P, PACK, P, PACK], BF16, name)
            copy(
                grouped[:].rearrange("p t q j -> p q j t"),
                raw[:].rearrange("p j (q t) -> p q j t", t=PACK),
            )
            return grouped

        def quantize_weight(grouped, name):
            codes = kept([P, H], U32, name + "_codes")
            scales = kept([P, H], U8, name + "_scales")
            nc.vector.quantize_mx(
                out=codes[:].bitcast(FP8X4), scales=scales[:], in_=grouped[:].rearrange("p t q j -> p (t q j)")
            )
            return codes, scales

        w4_codes = kept([P, PASSES, 2 * H], U8, "w4_codes")
        nc.vector.tensor_copy(
            w4_codes[:].bitcast(U16).rearrange("p a (t q) -> p a t q", t=PACK),
            w4_raw[:].bitcast(U16).rearrange("p a (q t) -> p a t q", t=PACK),
        )
        w1_bf = [round_weight(w1_raw[a], "w1_bf%d" % a, nc.scalar.copy) for a in range(PASSES)]
        packed_planes = (v_sc[:], v_sc[4:P, :])
        low_planes = (v_sc[:], v_sc_low[:])
        w1_q = [quantize_weight(w1_bf[a], "w1_%d" % a) for a in range(PASSES)]

        w4_dealt = kept([P, PASSES, H], U8, "w4_dealt")
        nc.vector.tensor_copy(
            w4_dealt[:].rearrange("p a (t q) -> p a t q", t=PACK),
            w4_sc[:].rearrange("p a (q t) -> p a t q", t=PACK),
        )
        v2_sc = gather(tab2_sc[:], offs2_sb[:], S2, U8, "v2_sc")
        w3_q = [quantize_weight(round_weight(w3_raw[0], "w3_bf0", nc.scalar.copy), "w3_0")]

        def gather_words(a):
            return [
                gather(
                    tab_w[a][:].bitcast(U32),
                    offs_sb[:, half * HALF // 16 : (half + 1) * HALF // 16],
                    HALF,
                    U32,
                    "v_w%d_%d" % (a, half),
                )
                for half in range(S // HALF)
            ]

        v_w = [gather_words(a) for a in range(PASSES)]
        w3_late = round_weight(w3_raw[1], "w3_bf1", nc.vector.tensor_copy)

        def fp8_weight(w_q):
            def pick(a, t):
                codes, scales = w_q[a]
                cols = slice(t * P, (t + 1) * P)
                return codes[:, cols].bitcast(FP8X4), scales[:, cols]

            return pick

        def fp4_weight(a, t):
            return (
                w4_codes[:, a, 2 * t * P : 2 * (t + 1) * P].bitcast(FP4X4),
                w4_dealt[:, a, t * P : (t + 1) * P],
            )

        def first_product(pick, planes, u):
            acc = psum.tile([P, PACK, UNIT], F32, name="acc", tag="bank")
            half, first = divmod(u * UNIT, HALF)
            for a in range(PASSES):
                for t in range(PACK):
                    codes, scales = pick(a, t)
                    nc.tensor.matmul_mx(
                        out=acc[:, t, :],
                        lhsT=codes,
                        lhsT_scale=scales,
                        rhs=v_w[a][half][:, first : first + UNIT].bitcast(FP8X4),
                        rhs_scale=planes[a][:, u * UNIT : (u + 1) * UNIT],
                        start=(a == 0 and t == 0),
                        stop=(a == PASSES - 1 and t == PACK - 1),
                    )
            return acc[:].rearrange("p t n -> p n t")

        def woven(tile):
            return tile[:].rearrange("p (n t) -> p n t", t=PACK)

        h_codes = kept([P, S], U32, "h_codes")
        h_scales = kept([P, S], U8, "h_scales")
        h_bf = kept([P, PACK * S], BF16, "h_bf")
        left, right = {}, {}

        def steer(u):
            s_acc = first_product(fp8_weight(w1_q), packed_planes, u)
            b_acc = first_product(fp4_weight, low_planes, u)
            left[u] = kept([P, PACK * UNIT], F32, "left%d" % u)
            right[u] = kept([P, PACK * UNIT], F32, "right%d" % u)
            nc.scalar.activation(woven(left[u]), s_acc, ACT.Tanh)
            nc.scalar.activation(woven(right[u]), s_acc, ACT.Abs)
            nc.vector.tensor_tensor(woven(left[u]), b_acc, woven(left[u]), ALU.mult)

        def scale_right(u):
            d_acc = first_product(fp8_weight(w3_q), packed_planes, u)
            nc.vector.tensor_tensor(woven(right[u]), d_acc, woven(right[u]), ALU.mult)

        def add_terms(u, engine):
            engine.tensor_tensor(h_bf[:, PACK * u * UNIT : PACK * (u + 1) * UNIT], left[u][:], right[u][:], ALU.add)

        def quantize_h(first, last):
            cols = slice(first * UNIT, last * UNIT)
            nc.vector.quantize_mx(
                out=h_codes[:, cols].bitcast(FP8X4),
                scales=h_scales[:, cols],
                in_=h_bf[:, PACK * cols.start : PACK * cols.stop],
            )

        LEAD = 2
        POOL_UNITS = 6
        steer(0)
        w3_q.append(quantize_weight(w3_late, "w3_1"))
        for u in range(1, LEAD):
            steer(u)
        v2_first = gather(tab2_w[:].bitcast(U32), offs2_sb[:, 0:16], 256, U32, "v2_first")
        for u in range(UNITS):
            if u + LEAD < UNITS:
                steer(u + LEAD)
            scale_right(u)
            if u < POOL_UNITS:
                add_terms(u, nc.gpsimd)
        quantize_h(0, 4)
        add_terms(6, nc.vector)
        add_terms(7, nc.vector)
        quantize_h(4, 6)
        quantize_h(6, 7)
        quantize_h(7, 8)
        v2_mid = gather(tab2_w[:].bitcast(U32), offs2_sb[:, 16:48], 512, U32, "v2_mid", "v_w1_1")
        v2_last = gather(tab2_w[:].bitcast(U32), offs2_sb[:, 48:64], 256, U32, "v2_last", "v_w0_1")

        def scores(m):
            e_sb = ring.tile([P, S], F32, name="e_sb")
            if m < 2:
                lhs = v2_first[:, m * P : (m + 1) * P]
            elif m < 6:
                lhs = v2_mid[:, (m - 2) * P : (m - 1) * P]
            else:
                lhs = v2_last[:, (m - 6) * P : (m - 5) * P]
            edges = (0, 512, 768, 896, 1024) if m == 0 else (0, 512, 1024)
            for first, last in zip(edges, edges[1:]):
                cols = slice(first, last)
                acc = psum.tile([P, last - first], F32, name="e_acc", tag="bank")
                nc.tensor.matmul_mx(
                    out=acc[:],
                    lhsT=lhs.bitcast(FP8X4),
                    lhsT_scale=v2_sc[8:P, m * P : (m + 1) * P],
                    rhs=h_codes[:, cols].bitcast(FP8X4),
                    rhs_scale=h_scales[:, cols],
                    start=True,
                    stop=True,
                )
                nc.scalar.copy(e_sb[:, cols], acc[:])
            return e_sb

        def finish(m, floored, evening, cols):
            best = ring.tile([P, cols.stop - cols.start], F32, name="best")
            nc.vector.tensor_tensor(best[:], floored[:, cols], evening[:], ALU.max)
            nc.sync.dma_start(out=out[m * P : (m + 1) * P, cols], in_=best[:])

        def pick(e_sb, pos_sb, cols, name):
            picked = ring.tile([P, cols.stop - cols.start], F32, name=name)
            nc.vector.tensor_copy(picked[:], e_sb[:].indirect(pos_sb[:, cols.start // 16 : cols.stop // 16]))
            return picked

        whole = slice(0, J)
        pending = None
        for m in range(ROW_TILES):
            e_sb = scores(m)
            morning = pick(e_sb, pos1_sb, whole, "morning")
            if pending is not None:
                finish(*pending)
            floored = ring.tile([P, J], F32, name="floored")
            nc.vector.tensor_tensor(floored[:], morning[:], amin_sb[m // 4][:, m % 4, :], ALU.max)
            if m < ROW_TILES - 1:
                pending = (m, floored, pick(e_sb, pos2_sb, whole, "evening"), whole)
            else:
                halves = (slice(0, J // 2), slice(J // 2, J))
                evenings = [pick(e_sb, pos2_sb, cols, "evening") for cols in halves]
                for cols, evening in zip(halves, evenings):
                    finish(m, floored, evening, cols)
